import numpy as np
import ml_dtypes


def mxq(x, axis, fmt="e4m3"):
    dtype, down = {"e4m3": (ml_dtypes.float8_e4m3fn, 7), "e5m2": (ml_dtypes.float8_e5m2, 14)}[fmt]
    v = np.moveaxis(np.asarray(x, np.float32).astype(ml_dtypes.bfloat16).astype(np.float64), axis, -1)
    blocks = v.reshape(v.shape[:-1] + (-1, 32))
    amax = np.abs(blocks).max(-1, keepdims=True)
    byte = np.maximum(np.where(amax > 0, np.frexp(amax)[1] - 1 + 127, 0) - down, 1)
    scale = np.exp2(byte - 127.0)
    codes = (blocks / scale).astype(np.float32).astype(dtype).astype(np.float64)
    return np.moveaxis((codes * scale).reshape(v.shape), -1, axis)


WIDE = False


def mx_kscale(k):
    if not WIDE:
        return np.ones(k)
    levels = np.array([10, -10, 5, -5, 0])
    if k % 512:
        return np.exp2(np.random.permutation(np.resize(levels, k // 32))).repeat(32)
    a = np.empty((k // 512, 16))
    for p in range(k // 512):
        a[p, :8] = np.random.permutation(np.resize(levels, 8))
        for g in range(8):
            far = levels[np.abs(levels - a[p, g]) >= 10]
            a[p, g + 8] = far[np.random.randint(len(far))]
    return np.exp2(a.ravel()).repeat(32)


def f64(x):
    return np.asarray(x).astype(np.float64)


def striped(idx):
    return np.tile(idx.reshape(-1, 16).T, (8, 1)).astype(np.uint16)


def unstriped(offs):
    return offs[:16].T.reshape(-1).astype(np.int64)


E2M1 = np.array([0.0, 0.5, 1.0, 1.5, 2.0, 3.0, 4.0, 6.0, -0.0, -0.5, -1.0, -1.5, -2.0, -3.0, -4.0, -6.0])


def pack_weight(w, fmt):
    k, n = w.shape
    w = f64(np.asarray(w, np.float32).astype(ml_dtypes.bfloat16)).reshape(k // 32, 32, n)
    amax = np.abs(w).max(1)
    if fmt == "e4m3":
        byte = np.frexp(amax)[1] - 1 + 127 - 7
    else:
        mant, ex = np.frexp(amax / 6.0)
        byte = np.where(mant > 0.5, ex, ex - 1) + 127
    byte = np.clip(np.where(amax > 0, byte, 1), 1, 254)
    scaled = (w * np.exp2(127.0 - byte)[:, None, :]).reshape(k, n).astype(np.float32)
    by_word = np.ascontiguousarray(scaled.reshape(k // 512, 128, 4, n).transpose(0, 1, 3, 2))
    if fmt == "e4m3":
        words = by_word.astype(ml_dtypes.float8_e4m3fn).view(np.uint8)
    else:
        c = by_word.astype(ml_dtypes.float4_e2m1fn).view(np.uint8) & 0xF
        words = (c[..., 0::2] | (c[..., 1::2] << 4)).reshape(k // 512, 128, 2 * n)
    return np.ascontiguousarray(words), np.ascontiguousarray(byte.astype(np.uint8).reshape(k // 512, 16, n))


def unpack_weight(words, scales, fmt):
    g, _, n = scales.shape
    words = np.ascontiguousarray(words).reshape(g, 128, n, -1)
    if fmt == "e4m3":
        vals = words.view(ml_dtypes.float8_e4m3fn).astype(np.float64)
    else:
        nib = np.empty((g, 128, n, 4), np.uint8)
        nib[..., 0::2] = words & 0xF
        nib[..., 1::2] = words >> 4
        vals = E2M1[nib]
    vals = vals * np.repeat(np.exp2(scales.astype(np.float64) - 127.0), 8, axis=1)[..., None]
    return vals.transpose(0, 1, 3, 2).reshape(g * 512, n)


K, T, E, C, N = 2048, 1280, 6, 128, 128


def by_expert(wq, xq):
    return np.concatenate([wq[e].T @ xq[:, e * C:(e + 1) * C] for e in range(E)], axis=1)


def setup_inputs():
    n = np.random.standard_normal
    s = mx_kscale(K)[:, None]
    x = pack_weight(n((K, T)) * s, "e4m3")
    return {
        "x_words": x[0],
        "x_scales": x[1],
        "w": (n((E, K, N)) / np.sqrt(K) / s[None]).astype(np.float32),
        "gate": np.tile(np.random.uniform(0.2, 1.0, E * C), (N, 1)).astype(np.float32),
        "offs": striped(np.random.permutation(T)[:E * C]),
        "dst": striped(np.random.permutation(T)[:E * C]),
    }


def reference(x_words, x_scales, w, gate, offs, dst):
    idx = unstriped(offs)
    xq = unpack_weight(x_words, x_scales, "e4m3")[:, idx]
    y = by_expert(mxq(f64(w), 1, "e4m3"), xq)
    out = np.zeros((N, T))
    out[:, unstriped(dst)] = f64(gate) * y
    return out

@@ -1,0 +1,139 @@
+from contextlib import ExitStack
+
+import concourse.mybir as mybir
+
+K, T, E, C, N = 2048, 1280, 6, 128, 128
+S = E * C
+FLOPS = 2 * K * N * S
+
+F32 = mybir.dt.float32
+BF16 = mybir.dt.bfloat16
+I32 = mybir.dt.int32
+U32 = mybir.dt.uint32
+U16 = mybir.dt.uint16
+U8 = mybir.dt.uint8
+FP8X4 = mybir.dt.float8_e4m3fn_x4
+MULT = mybir.AluOpType.mult
+
+P = 128
+PACK = 4
+K_PASS = P * PACK
+PASSES = K // K_PASS
+RUN = 4
+PER_COLUMN = 16
+
+CHUNKS = [(e, a, 2) for e in range(E - 1) for a in (0, 2)] + [(E - 1, 0, 2), (E - 1, 2, 1), (E - 1, 3, 1)]
+VECTOR_WORDS = {10: 128, 11: 64}
+GATE_CUT = 512
+SCATTER_BEFORE = {7: 0, 11: 1}
+SCATTER_CUTS = [0, 384, 608, 768]
+
+
+def tile_moe_two_lin_none_kernel(tc, x_words, x_scales, w, gate, offs, dst, out):
+    nc = tc.nc
+    with ExitStack() as ctx:
+        keep = ctx.enter_context(tc.tile_pool(name="keep", bufs=1))
+        psum = ctx.enter_context(tc.psum_pool(name="psum", bufs=1))
+
+        offs_sb = keep.tile([P, S // PER_COLUMN], U16, name="offs_sb")
+        dst_sb = keep.tile([P, S // PER_COLUMN], U16, name="dst_sb")
+        tok_words = [keep.tile([P, T], I32, name="tok_words%d" % a, align_bytes=64) for a in range(PASSES)]
+        tok_scales = keep.tile([P, T], U8, name="tok_scales", align_bytes=64)
+        slot_words = [keep.tile([P, S], U32, name="slot_words%d" % a, align_bytes=64) for a in range(PASSES)]
+        slot_scales = keep.tile([P, S], U8, name="slot_scales", align_bytes=64)
+        gate_sb = keep.tile([P, S], F32, name="gate_sb", align_bytes=64)
+        y_sb = keep.tile([P, S], F32, name="y_sb", align_bytes=64)
+        out_sb = keep.tile([P, T], F32, name="out_sb", align_bytes=64)
+        w_raw = [keep.tile([P, n, PACK, N], F32, name="w_raw%d" % i, align_bytes=64) for i, (e, a, n) in enumerate(CHUNKS)]
+        w_bf = [keep.tile([P, n, N, PACK], BF16, name="w_bf%d" % i, align_bytes=64) for i, (e, a, n) in enumerate(CHUNKS)]
+        w_codes = [keep.tile([P, n * N], U32, name="w_codes%d" % i, align_bytes=64) for i, (e, a, n) in enumerate(CHUNKS)]
+        w_scales = [keep.tile([P, n * N], U8, name="w_scales%d" % i, align_bytes=64) for i, (e, a, n) in enumerate(CHUNKS)]
+        acc = [psum.tile([P, C], F32, name="acc%d" % e) for e in range(E)]
+
+        def load_tokens(a):
+            nc.sync.dma_start(out=tok_words[a][:], in_=x_words[a].rearrange("p t r -> p (t r)").bitcast(I32))
+
+        def load_chunk(i):
+            e, a, n = CHUNKS[i]
+            rows = w[e, a * K_PASS : (a + n) * K_PASS, :]
+            nc.sync.dma_start(out=w_raw[i][:], in_=rows.rearrange("(o p j) n -> p o j n", o=n, j=PACK))
+
+        def gather_words(a):
+            nc.vector.tensor_copy(slot_words[a][:], tok_words[a][:].bitcast(U32).indirect(offs_sb[:]))
+
+        def cast_chunk(i):
+            e, a, n = CHUNKS[i]
+            src = w_raw[i][:].rearrange("p o j (c i) -> p o c j i", i=RUN)
+            to = w_bf[i][:].rearrange("p o (c i) j -> p o c j i", i=RUN)
+            cut = VECTOR_WORDS.get(i, 0)
+            if n == 1:
+                src, to, cut, end = src[:, 0], to[:, 0], cut // RUN, N // RUN
+            else:
+                cut, end = cut // N, n
+            if cut > 0:
+                nc.vector.tensor_copy(out=to[:, :cut], in_=src[:, :cut])
+            if cut < end:
+                nc.scalar.copy(out=to[:, cut:], in_=src[:, cut:])
+
+        def quantize_chunk(i):
+            nc.vector.quantize_mx(
+                out=w_codes[i][:].bitcast(FP8X4),
+                scales=w_scales[i][:],
+                in_=w_bf[i][:].rearrange("p o n j -> p (o n j)"),
+            )
+
+        def multiply_chunk(i):
+            e, a, n = CHUNKS[i]
+            slots = slice(e * C, (e + 1) * C)
+            for o in range(n):
+                cols = slice(o * N, (o + 1) * N)
+                nc.tensor.matmul_mx(
+                    out=acc[e][:],
+                    lhsT=w_codes[i][:, cols].bitcast(FP8X4),
+                    lhsT_scale=w_scales[i][:, cols],
+                    rhs=slot_words[a + o][:, slots].bitcast(FP8X4),
+                    rhs_scale=slot_scales[4 * (a + o) :, slots],
+                    start=(a + o == 0),
+                    stop=(a + o == PASSES - 1),
+                )
+            if a + n == PASSES:
+                nc.vector.tensor_tensor(y_sb[:, slots], acc[e][:], gate_sb[:, slots], MULT)
+
+        def scatter(u):
+            lo, hi = SCATTER_CUTS[u], SCATTER_CUTS[u + 1]
+            places = dst_sb[:, lo // PER_COLUMN : hi // PER_COLUMN]
+            nc.vector.tensor_copy(out_sb[:].indirect(places), y_sb[:, lo:hi])
+
+        nc.vector.memset(tok_scales[:].bitcast(I32), 0)
+        for q in range(4):
+            nc.scalar.dma_start(
+                out=tok_scales[32 * q : 32 * q + 16, :].bitcast(I32),
+                in_=x_scales[:, 4 * q : 4 * q + 4, :].bitcast(I32),
+            )
+        nc.vector.memset(out_sb[:], 0.0)
+
+        nc.sync.dma_start(offs_sb[:], offs)
+        load_tokens(0)
+        load_tokens(1)
+        load_chunk(0)
+        load_tokens(2)
+        nc.sync.dma_start(dst_sb[:], dst)
+        load_chunk(1)
+        load_tokens(3)
+        for i in range(2, len(CHUNKS)):
+            if i == 8:
+                nc.sync.dma_start(out=gate_sb[:, :GATE_CUT], in_=gate[:, :GATE_CUT])
+            load_chunk(i)
+        nc.sync.dma_start(out=gate_sb[:, GATE_CUT:], in_=gate[:, GATE_CUT:])
+
+        nc.vector.tensor_copy(slot_scales[:], tok_scales[:].indirect(offs_sb[:]))
+        for a in range(PASSES):
+            gather_words(a)
+        for i in range(len(CHUNKS)):
+            if i in SCATTER_BEFORE:
+                scatter(SCATTER_BEFORE[i])
+            cast_chunk(i)
+            quantize_chunk(i)
+            multiply_chunk(i)
+        scatter(len(SCATTER_CUTS) - 2)
+        nc.sync.dma_start(out=out, in_=out_sb[:])

@@ -22,11 +22,11 @@ PASSES = K // K_PASS
 RUN = 4
 PER_COLUMN = 16
 
-CHUNKS = [(e, a, 2) for e in range(E - 1) for a in (0, 2)] + [(E - 1, 0, 2), (E - 1, 2, 1), (E - 1, 3, 1)]
-VECTOR_WORDS = {10: 128, 11: 64}
-GATE_CUT = 512
-SCATTER_BEFORE = {7: 0, 11: 1}
-SCATTER_CUTS = [0, 384, 608, 768]
+CHUNKS = [(0, 0, 2),(0, 2, 2),(1, 0, 2),(1, 2, 2),(2, 0, 2),(2, 2, 2),(3, 0, 2),(3, 2, 2),(4, 0, 2),(4, 2, 2),(5, 0, 1),(5, 1, 1),(5, 2, 1),(5, 3, 1)]
+LOADS = [("offs",), ("tokens", 0, 1), ("tokens", 1, 1), ("w", 0, 1), ("tokens", 2, 2), ("w", 1, 1), ("dst",), ("w", 2, 2), ("w", 4, 2), ("w", 6, 1), ("gate", 0, 384), ("w", 7, 1), ("w", 8, 1), ("w", 9, 1), ("w", 10, 1), ("w", 11, 1), ("gate", 384, 512), ("w", 12, 1), ("w", 13, 1), ("gate", 512, 768)]
+VECTOR_WORDS = {2: 128, 4: 256, 6: 128, 10: 128}
+SCATTER_BEFORE = {7: [0], 9: [1], 12: [2]}
+SCATTER_CUTS = [0,288,448,608,768]
 
 
 def tile_moe_two_lin_none_kernel(tc, x_words, x_scales, w, gate, offs, dst, out):
@@ -37,33 +37,41 @@ def tile_moe_two_lin_none_kernel(tc, x_words, x_scales, w, gate, offs, dst, out)
 
         offs_sb = keep.tile([P, S // PER_COLUMN], U16, name="offs_sb")
         dst_sb = keep.tile([P, S // PER_COLUMN], U16, name="dst_sb")
-        tok_words = [keep.tile([P, T], I32, name="tok_words%d" % a, align_bytes=64) for a in range(PASSES)]
+        tok_words = {}
         tok_scales = keep.tile([P, T], U8, name="tok_scales", align_bytes=64)
         slot_words = [keep.tile([P, S], U32, name="slot_words%d" % a, align_bytes=64) for a in range(PASSES)]
         slot_scales = keep.tile([P, S], U8, name="slot_scales", align_bytes=64)
         gate_sb = keep.tile([P, S], F32, name="gate_sb", align_bytes=64)
         y_sb = keep.tile([P, S], F32, name="y_sb", align_bytes=64)
         out_sb = keep.tile([P, T], F32, name="out_sb", align_bytes=64)
-        w_raw = [keep.tile([P, n, PACK, N], F32, name="w_raw%d" % i, align_bytes=64) for i, (e, a, n) in enumerate(CHUNKS)]
+        w_raw = {}
         w_bf = [keep.tile([P, n, N, PACK], BF16, name="w_bf%d" % i, align_bytes=64) for i, (e, a, n) in enumerate(CHUNKS)]
         w_codes = [keep.tile([P, n * N], U32, name="w_codes%d" % i, align_bytes=64) for i, (e, a, n) in enumerate(CHUNKS)]
         w_scales = [keep.tile([P, n * N], U8, name="w_scales%d" % i, align_bytes=64) for i, (e, a, n) in enumerate(CHUNKS)]
         acc = [psum.tile([P, C], F32, name="acc%d" % e) for e in range(E)]
 
-        def load_tokens(a):
-            nc.sync.dma_start(out=tok_words[a][:], in_=x_words[a].rearrange("p t r -> p (t r)").bitcast(I32))
+        def load_tokens(first, count):
+            tile = keep.tile([P, count, T], I32, name="tok_words%d" % first, align_bytes=64)
+            rows = x_words[first : first + count].rearrange("o p t r -> p o (t r)")
+            nc.sync.dma_start(out=tile[:], in_=rows.bitcast(I32))
+            for o in range(count):
+                tok_words[first + o] = tile[:, o, :]
 
-        def load_chunk(i):
-            e, a, n = CHUNKS[i]
-            rows = w[e, a * K_PASS : (a + n) * K_PASS, :]
-            nc.sync.dma_start(out=w_raw[i][:], in_=rows.rearrange("(o p j) n -> p o j n", o=n, j=PACK))
+        def load_w(first, count):
+            e, a, n = CHUNKS[first]
+            passes = sum(CHUNKS[i][2] for i in range(first, first + count))
+            tile = keep.tile([P, passes, PACK, N], F32, name="w_raw%d" % first, align_bytes=64)
+            rows = w[e, a * K_PASS : (a + passes) * K_PASS, :]
+            nc.sync.dma_start(out=tile[:], in_=rows.rearrange("(o p j) n -> p o j n", o=passes, j=PACK))
+            for i in range(first, first + count):
+                w_raw[i] = tile[:, CHUNKS[i][1] - a : CHUNKS[i][1] - a + CHUNKS[i][2]]
 
         def gather_words(a):
-            nc.vector.tensor_copy(slot_words[a][:], tok_words[a][:].bitcast(U32).indirect(offs_sb[:]))
+            nc.vector.tensor_copy(slot_words[a][:], tok_words[a].bitcast(U32).indirect(offs_sb[:]))
 
         def cast_chunk(i):
             e, a, n = CHUNKS[i]
-            src = w_raw[i][:].rearrange("p o j (c i) -> p o c j i", i=RUN)
+            src = w_raw[i].rearrange("p o j (c i) -> p o c j i", i=RUN)
             to = w_bf[i][:].rearrange("p o (c i) j -> p o c j i", i=RUN)
             cut = VECTOR_WORDS.get(i, 0)
             if n == 1:
@@ -112,26 +120,24 @@ def tile_moe_two_lin_none_kernel(tc, x_words, x_scales, w, gate, offs, dst, out)
             )
         nc.vector.memset(out_sb[:], 0.0)
 
-        nc.sync.dma_start(offs_sb[:], offs)
-        load_tokens(0)
-        load_tokens(1)
-        load_chunk(0)
-        load_tokens(2)
-        nc.sync.dma_start(dst_sb[:], dst)
-        load_chunk(1)
-        load_tokens(3)
-        for i in range(2, len(CHUNKS)):
-            if i == 8:
-                nc.sync.dma_start(out=gate_sb[:, :GATE_CUT], in_=gate[:, :GATE_CUT])
-            load_chunk(i)
-        nc.sync.dma_start(out=gate_sb[:, GATE_CUT:], in_=gate[:, GATE_CUT:])
+        for load in LOADS:
+            if load[0] == "offs":
+                nc.sync.dma_start(offs_sb[:], offs)
+            elif load[0] == "dst":
+                nc.sync.dma_start(dst_sb[:], dst)
+            elif load[0] == "tokens":
+                load_tokens(load[1], load[2])
+            elif load[0] == "w":
+                load_w(load[1], load[2])
+            else:
+                nc.sync.dma_start(out=gate_sb[:, load[1] : load[2]], in_=gate[:, load[1] : load[2]])
 
         nc.vector.tensor_copy(slot_scales[:], tok_scales[:].indirect(offs_sb[:]))
         for a in range(PASSES):
             gather_words(a)
         for i in range(len(CHUNKS)):
-            if i in SCATTER_BEFORE:
-                scatter(SCATTER_BEFORE[i])
+            for u in SCATTER_BEFORE.get(i, []):
+                scatter(u)
             cast_chunk(i)
             quantize_chunk(i)
             multiply_chunk(i)

@@ -23,10 +23,10 @@ RUN = 4
 PER_COLUMN = 16
 
 CHUNKS = [(0, 0, 2),(0, 2, 2),(1, 0, 2),(1, 2, 2),(2, 0, 2),(2, 2, 2),(3, 0, 2),(3, 2, 2),(4, 0, 2),(4, 2, 2),(5, 0, 1),(5, 1, 1),(5, 2, 1),(5, 3, 1)]
-LOADS = [("offs",), ("tokens", 0, 1), ("tokens", 1, 1), ("w", 0, 1), ("tokens", 2, 2), ("w", 1, 1), ("dst",), ("w", 2, 2), ("w", 4, 2), ("w", 6, 1), ("gate", 0, 384), ("w", 7, 1), ("w", 8, 1), ("w", 9, 1), ("w", 10, 1), ("w", 11, 1), ("gate", 384, 512), ("w", 12, 1), ("w", 13, 1), ("gate", 512, 768)]
-VECTOR_WORDS = {2: 128, 4: 256, 6: 128, 10: 128}
-SCATTER_BEFORE = {7: [0], 9: [1], 12: [2]}
-SCATTER_CUTS = [0,288,448,608,768]
+LOADS = [("offs",), ("tokens", 0, 1), ("scales",), ("w", 0, 2), ("tokens", 1, 1), ("tokens", 2, 1), ("w", 2, 2), ("tokens", 3, 1), ("dst",), ("w", 4, 1), ("w", 5, 1), ("gate", 0, 256), ("w", 6, 1), ("w", 7, 1), ("w", 8, 1), ("w", 9, 1), ("w", 10, 1), ("gate", 256, 512), ("w", 11, 1), ("w", 12, 1), ("w", 13, 1), ("gate", 512, 768)]
+VECTOR_WORDS = {5: 128, 7: 128, 9: 128}
+SCATTER_BEFORE = {5: [0], 8: [1], 10: [2]}
+SCATTER_CUTS = [0,256,416,608,768]
 
 
 def tile_moe_two_lin_none_kernel(tc, x_words, x_scales, w, gate, offs, dst, out):
@@ -113,11 +113,6 @@ def tile_moe_two_lin_none_kernel(tc, x_words, x_scales, w, gate, offs, dst, out)
             nc.vector.tensor_copy(out_sb[:].indirect(places), y_sb[:, lo:hi])
 
         nc.vector.memset(tok_scales[:].bitcast(I32), 0)
-        for q in range(4):
-            nc.scalar.dma_start(
-                out=tok_scales[32 * q : 32 * q + 16, :].bitcast(I32),
-                in_=x_scales[:, 4 * q : 4 * q + 4, :].bitcast(I32),
-            )
         nc.vector.memset(out_sb[:], 0.0)
 
         for load in LOADS:
@@ -125,6 +120,12 @@ def tile_moe_two_lin_none_kernel(tc, x_words, x_scales, w, gate, offs, dst, out)
                 nc.sync.dma_start(offs_sb[:], offs)
             elif load[0] == "dst":
                 nc.sync.dma_start(dst_sb[:], dst)
+            elif load[0] == "scales":
+                for q in range(4):
+                    nc.sync.dma_start(
+                        out=tok_scales[32 * q : 32 * q + 16, :].bitcast(I32),
+                        in_=x_scales[:, 4 * q : 4 * q + 4, :].bitcast(I32),
+                    )
             elif load[0] == "tokens":
                 load_tokens(load[1], load[2])
             elif load[0] == "w":

@@ -23,10 +23,10 @@ RUN = 4
 PER_COLUMN = 16
 
 CHUNKS = [(0, 0, 2),(0, 2, 2),(1, 0, 2),(1, 2, 2),(2, 0, 2),(2, 2, 2),(3, 0, 2),(3, 2, 2),(4, 0, 2),(4, 2, 2),(5, 0, 1),(5, 1, 1),(5, 2, 1),(5, 3, 1)]
-LOADS = [("offs",), ("tokens", 0, 1), ("scales",), ("w", 0, 2), ("tokens", 1, 1), ("tokens", 2, 1), ("w", 2, 2), ("tokens", 3, 1), ("dst",), ("w", 4, 1), ("w", 5, 1), ("gate", 0, 256), ("w", 6, 1), ("w", 7, 1), ("w", 8, 1), ("w", 9, 1), ("w", 10, 1), ("gate", 256, 512), ("w", 11, 1), ("w", 12, 1), ("w", 13, 1), ("gate", 512, 768)]
-VECTOR_WORDS = {5: 128, 7: 128, 9: 128}
-SCATTER_BEFORE = {5: [0], 8: [1], 10: [2]}
-SCATTER_CUTS = [0,256,416,608,768]
+LOADS = [("offs",), ("tokens", 0, 1), ("scales",), ("w", 0, 2), ("tokens", 1, 1), ("tokens", 2, 1), ("w", 2, 2), ("tokens", 3, 1), ("dst",), ("w", 4, 1), ("w", 5, 1), ("gate", 0, 256), ("w", 6, 1), ("w", 7, 1), ("w", 8, 1), ("w", 9, 1), ("gate", 256, 512), ("w", 10, 1), ("w", 11, 1), ("w", 12, 1), ("w", 13, 1), ("gate", 512, 768)]
+VECTOR_WORDS = {7: 128, 9: 128}
+SCATTER_BEFORE = {5: [0], 8: [1], 11: [2]}
+SCATTER_CUTS = [0,256,448,608,768]
 
 
 def tile_moe_two_lin_none_kernel(tc, x_words, x_scales, w, gate, offs, dst, out):
@@ -105,12 +105,22 @@ def tile_moe_two_lin_none_kernel(tc, x_words, x_scales, w, gate, offs, dst, out)
                     stop=(a + o == PASSES - 1),
                 )
             if a + n == PASSES:
-                nc.vector.tensor_tensor(y_sb[:, slots], acc[e][:], gate_sb[:, slots], MULT)
+                lo, hi = e * C, (e + 1) * C
+                cut = min(max(SCATTER_CUTS[-2], lo), hi)
+                if cut > lo:
+                    nc.vector.tensor_tensor(y_sb[:, lo:cut], acc[e][:, : cut - lo], gate_sb[:, lo:cut], MULT)
+                if cut == lo:
+                    nc.scalar.copy(out=y_sb[:, lo:hi], in_=acc[e][:])
+                elif cut < hi:
+                    nc.vector.tensor_copy(out=y_sb[:, cut:hi], in_=acc[e][:, cut - lo :])
 
         def scatter(u):
             lo, hi = SCATTER_CUTS[u], SCATTER_CUTS[u + 1]
             places = dst_sb[:, lo // PER_COLUMN : hi // PER_COLUMN]
-            nc.vector.tensor_copy(out_sb[:].indirect(places), y_sb[:, lo:hi])
+            if hi < S:
+                nc.vector.tensor_copy(out_sb[:].indirect(places), y_sb[:, lo:hi])
+            else:
+                nc.vector.tensor_tensor(out_sb[:].indirect(places), y_sb[:, lo:hi], gate_sb[:, lo:hi], MULT)
 
         nc.vector.memset(tok_scales[:].bitcast(I32), 0)
         nc.vector.memset(out_sb[:], 0.0)

from contextlib import ExitStack

import concourse.mybir as mybir

K, T, E, C, N = 2048, 1280, 6, 128, 128
S = E * C
FLOPS = 2 * K * N * S

F32 = mybir.dt.float32
BF16 = mybir.dt.bfloat16
I32 = mybir.dt.int32
U32 = mybir.dt.uint32
U16 = mybir.dt.uint16
U8 = mybir.dt.uint8
FP8X4 = mybir.dt.float8_e4m3fn_x4
MULT = mybir.AluOpType.mult

P = 128
PACK = 4
K_PASS = P * PACK
PASSES = K // K_PASS
RUN = 4
PER_COLUMN = 16

CHUNKS = [(0, 0, 2),(0, 2, 2),(1, 0, 2),(1, 2, 2),(2, 0, 2),(2, 2, 2),(3, 0, 2),(3, 2, 2),(4, 0, 2),(4, 2, 2),(5, 0, 1),(5, 1, 1),(5, 2, 1),(5, 3, 1)]
LOADS = [("offs",), ("tokens", 0, 1), ("scales",), ("w", 0, 2), ("tokens", 1, 1), ("tokens", 2, 1), ("w", 2, 2), ("tokens", 3, 1), ("dst",), ("w", 4, 1), ("w", 5, 1), ("gate", 0, 256), ("w", 6, 1), ("w", 7, 1), ("w", 8, 1), ("w", 9, 1), ("gate", 256, 512), ("w", 10, 1), ("w", 11, 1), ("w", 12, 1), ("w", 13, 1), ("gate", 512, 768)]
VECTOR_WORDS = {7: 128, 9: 128}
SCATTER_BEFORE = {5: [0], 8: [1], 11: [2]}
SCATTER_CUTS = [0,256,448,608,768]


def tile_moe_two_lin_none_kernel(tc, x_words, x_scales, w, gate, offs, dst, out):
    nc = tc.nc
    with ExitStack() as ctx:
        keep = ctx.enter_context(tc.tile_pool(name="keep", bufs=1))
        psum = ctx.enter_context(tc.psum_pool(name="psum", bufs=1))

        offs_sb = keep.tile([P, S // PER_COLUMN], U16, name="offs_sb")
        dst_sb = keep.tile([P, S // PER_COLUMN], U16, name="dst_sb")
        tok_words = {}
        tok_scales = keep.tile([P, T], U8, name="tok_scales", align_bytes=64)
        slot_words = [keep.tile([P, S], U32, name="slot_words%d" % a, align_bytes=64) for a in range(PASSES)]
        slot_scales = keep.tile([P, S], U8, name="slot_scales", align_bytes=64)
        gate_sb = keep.tile([P, S], F32, name="gate_sb", align_bytes=64)
        y_sb = keep.tile([P, S], F32, name="y_sb", align_bytes=64)
        out_sb = keep.tile([P, T], F32, name="out_sb", align_bytes=64)
        w_raw = {}
        w_bf = [keep.tile([P, n, N, PACK], BF16, name="w_bf%d" % i, align_bytes=64) for i, (e, a, n) in enumerate(CHUNKS)]
        w_codes = [keep.tile([P, n * N], U32, name="w_codes%d" % i, align_bytes=64) for i, (e, a, n) in enumerate(CHUNKS)]
        w_scales = [keep.tile([P, n * N], U8, name="w_scales%d" % i, align_bytes=64) for i, (e, a, n) in enumerate(CHUNKS)]
        acc = [psum.tile([P, C], F32, name="acc%d" % e) for e in range(E)]

        def load_tokens(first, count):
            tile = keep.tile([P, count, T], I32, name="tok_words%d" % first, align_bytes=64)
            rows = x_words[first : first + count].rearrange("o p t r -> p o (t r)")
            nc.sync.dma_start(out=tile[:], in_=rows.bitcast(I32))
            for o in range(count):
                tok_words[first + o] = tile[:, o, :]

        def load_w(first, count):
            e, a, n = CHUNKS[first]
            passes = sum(CHUNKS[i][2] for i in range(first, first + count))
            tile = keep.tile([P, passes, PACK, N], F32, name="w_raw%d" % first, align_bytes=64)
            rows = w[e, a * K_PASS : (a + passes) * K_PASS, :]
            nc.sync.dma_start(out=tile[:], in_=rows.rearrange("(o p j) n -> p o j n", o=passes, j=PACK))
            for i in range(first, first + count):
                w_raw[i] = tile[:, CHUNKS[i][1] - a : CHUNKS[i][1] - a + CHUNKS[i][2]]

        def gather_words(a):
            nc.vector.tensor_copy(slot_words[a][:], tok_words[a].bitcast(U32).indirect(offs_sb[:]))

        def cast_chunk(i):
            e, a, n = CHUNKS[i]
            src = w_raw[i].rearrange("p o j (c i) -> p o c j i", i=RUN)
            to = w_bf[i][:].rearrange("p o (c i) j -> p o c j i", i=RUN)
            cut = VECTOR_WORDS.get(i, 0)
            if n == 1:
                src, to, cut, end = src[:, 0], to[:, 0], cut // RUN, N // RUN
            else:
                cut, end = cut // N, n
            if cut > 0:
                nc.vector.tensor_copy(out=to[:, :cut], in_=src[:, :cut])
            if cut < end:
                nc.scalar.copy(out=to[:, cut:], in_=src[:, cut:])

        def quantize_chunk(i):
            nc.vector.quantize_mx(
                out=w_codes[i][:].bitcast(FP8X4),
                scales=w_scales[i][:],
                in_=w_bf[i][:].rearrange("p o n j -> p (o n j)"),
            )

        def multiply_chunk(i):
            e, a, n = CHUNKS[i]
            slots = slice(e * C, (e + 1) * C)
            for o in range(n):
                cols = slice(o * N, (o + 1) * N)
                nc.tensor.matmul_mx(
                    out=acc[e][:],
                    lhsT=w_codes[i][:, cols].bitcast(FP8X4),
                    lhsT_scale=w_scales[i][:, cols],
                    rhs=slot_words[a + o][:, slots].bitcast(FP8X4),
                    rhs_scale=slot_scales[4 * (a + o) :, slots],
                    start=(a + o == 0),
                    stop=(a + o == PASSES - 1),
                )
            if a + n == PASSES:
                lo, hi = e * C, (e + 1) * C
                cut = min(max(SCATTER_CUTS[-2], lo), hi)
                if cut > lo:
                    nc.vector.tensor_tensor(y_sb[:, lo:cut], acc[e][:, : cut - lo], gate_sb[:, lo:cut], MULT)
                if cut == lo:
                    nc.scalar.copy(out=y_sb[:, lo:hi], in_=acc[e][:])
                elif cut < hi:
                    nc.vector.tensor_copy(out=y_sb[:, cut:hi], in_=acc[e][:, cut - lo :])

        def scatter(u):
            lo, hi = SCATTER_CUTS[u], SCATTER_CUTS[u + 1]
            places = dst_sb[:, lo // PER_COLUMN : hi // PER_COLUMN]
            if hi < S:
                nc.vector.tensor_copy(out_sb[:].indirect(places), y_sb[:, lo:hi])
            else:
                nc.vector.tensor_tensor(out_sb[:].indirect(places), y_sb[:, lo:hi], gate_sb[:, lo:hi], MULT)

        nc.vector.memset(tok_scales[:].bitcast(I32), 0)
        nc.vector.memset(out_sb[:], 0.0)

        for load in LOADS:
            if load[0] == "offs":
                nc.sync.dma_start(offs_sb[:], offs)
            elif load[0] == "dst":
                nc.sync.dma_start(dst_sb[:], dst)
            elif load[0] == "scales":
                for q in range(4):
                    nc.sync.dma_start(
                        out=tok_scales[32 * q : 32 * q + 16, :].bitcast(I32),
                        in_=x_scales[:, 4 * q : 4 * q + 4, :].bitcast(I32),
                    )
            elif load[0] == "tokens":
                load_tokens(load[1], load[2])
            elif load[0] == "w":
                load_w(load[1], load[2])
            else:
                nc.sync.dma_start(out=gate_sb[:, load[1] : load[2]], in_=gate[:, load[1] : load[2]])

        nc.vector.tensor_copy(slot_scales[:], tok_scales[:].indirect(offs_sb[:]))
        for a in range(PASSES):
            gather_words(a)
        for i in range(len(CHUNKS)):
            for u in SCATTER_BEFORE.get(i, []):
                scatter(u)
            cast_chunk(i)
            quantize_chunk(i)
            multiply_chunk(i)
        scatter(len(SCATTER_CUTS) - 2)
        nc.sync.dma_start(out=out, in_=out_sb[:])
